import numpy as np
import ml_dtypes


def mxq(x, axis, fmt="e4m3"):
    dtype, down = {"e4m3": (ml_dtypes.float8_e4m3fn, 7), "e5m2": (ml_dtypes.float8_e5m2, 14)}[fmt]
    v = np.moveaxis(np.asarray(x, np.float32).astype(ml_dtypes.bfloat16).astype(np.float64), axis, -1)
    blocks = v.reshape(v.shape[:-1] + (-1, 32))
    amax = np.abs(blocks).max(-1, keepdims=True)
    byte = np.maximum(np.where(amax > 0, np.frexp(amax)[1] - 1 + 127, 0) - down, 1)
    scale = np.exp2(byte - 127.0)
    codes = (blocks / scale).astype(np.float32).astype(dtype).astype(np.float64)
    return np.moveaxis((codes * scale).reshape(v.shape), -1, axis)


WIDE = False


def mx_kscale(k):
    if not WIDE:
        return np.ones(k)
    levels = np.array([10, -10, 5, -5, 0])
    if k % 512:
        return np.exp2(np.random.permutation(np.resize(levels, k // 32))).repeat(32)
    a = np.empty((k // 512, 16))
    for p in range(k // 512):
        a[p, :8] = np.random.permutation(np.resize(levels, 8))
        for g in range(8):
            far = levels[np.abs(levels - a[p, g]) >= 10]
            a[p, g + 8] = far[np.random.randint(len(far))]
    return np.exp2(a.ravel()).repeat(32)


def f64(x):
    return np.asarray(x).astype(np.float64)


E2M1 = np.array([0.0, 0.5, 1.0, 1.5, 2.0, 3.0, 4.0, 6.0, -0.0, -0.5, -1.0, -1.5, -2.0, -3.0, -4.0, -6.0])


def pack_weight(w, fmt):
    k, n = w.shape
    w = f64(np.asarray(w, np.float32).astype(ml_dtypes.bfloat16)).reshape(k // 32, 32, n)
    amax = np.abs(w).max(1)
    if fmt == "e4m3":
        byte = np.frexp(amax)[1] - 1 + 127 - 7
    else:
        mant, ex = np.frexp(amax / 6.0)
        byte = np.where(mant > 0.5, ex, ex - 1) + 127
    byte = np.clip(np.where(amax > 0, byte, 1), 1, 254)
    scaled = (w * np.exp2(127.0 - byte)[:, None, :]).reshape(k, n).astype(np.float32)
    by_word = np.ascontiguousarray(scaled.reshape(k // 512, 128, 4, n).transpose(0, 1, 3, 2))
    if fmt == "e4m3":
        words = by_word.astype(ml_dtypes.float8_e4m3fn).view(np.uint8)
    else:
        c = by_word.astype(ml_dtypes.float4_e2m1fn).view(np.uint8) & 0xF
        words = (c[..., 0::2] | (c[..., 1::2] << 4)).reshape(k // 512, 128, 2 * n)
    return np.ascontiguousarray(words), np.ascontiguousarray(byte.astype(np.uint8).reshape(k // 512, 16, n))


def unpack_weight(words, scales, fmt):
    g, _, n = scales.shape
    words = np.ascontiguousarray(words).reshape(g, 128, n, -1)
    if fmt == "e4m3":
        vals = words.view(ml_dtypes.float8_e4m3fn).astype(np.float64)
    else:
        nib = np.empty((g, 128, n, 4), np.uint8)
        nib[..., 0::2] = words & 0xF
        nib[..., 1::2] = words >> 4
        vals = E2M1[nib]
    vals = vals * np.repeat(np.exp2(scales.astype(np.float64) - 127.0), 8, axis=1)[..., None]
    return vals.transpose(0, 1, 3, 2).reshape(g * 512, n)


K, M, T = 2048, 1024, 1024


def setup_inputs():
    n = np.random.standard_normal
    s = mx_kscale(K)[:, None]
    p_w4 = pack_weight(n((K, M)) / np.sqrt(K) / s, "e2m1")
    p_w8 = pack_weight(n((K, M)) / np.sqrt(K) / s, "e4m3")
    return {
        "x": (n((K, T)) * s).astype(np.float32),
        "w4_words": p_w4[0],
        "w4_scales": p_w4[1],
        "w8_words": p_w8[0],
        "w8_scales": p_w8[1],
        "b": (0.3 * n(1024)).astype(np.float32),
    }


def reference(x, w4_words, w4_scales, w8_words, w8_scales, b):
    xa_, xb_ = mxq(np.maximum(f64(x), 0.0), 0, "e4m3"), mxq(np.maximum(-f64(x), 0.0), 0, "e4m3")
    w4_ = unpack_weight(w4_words, w4_scales, "e2m1")
    w8_ = unpack_weight(w8_words, w8_scales, "e4m3")
    y = w4_.T @ xa_ + w8_.T @ xb_
    return y + f64(b)[:, None]

@@ -1,0 +1,228 @@
+from contextlib import ExitStack
+
+import concourse.mybir as mybir
+
+K, M, T = 2048, 1024, 1024
+FLOPS = 2 * 2 * K * M * T
+
+F32 = mybir.dt.float32
+BF16 = mybir.dt.bfloat16
+I32 = mybir.dt.int32
+U32 = mybir.dt.uint32
+U8 = mybir.dt.uint8
+FP8X4 = mybir.dt.float8_e4m3fn_x4
+FP4X4 = mybir.dt.float4_e2m1fn_x4
+ALU = mybir.AluOpType
+ACT = mybir.ActivationFunctionType
+
+P = 128
+PACK = 4
+K_PASS = P * PACK
+PASSES = K // K_PASS
+M_TILES = M // P
+N = 512
+HALF = N // 2
+SWEEPS = T // N
+STEPS = SWEEPS * PASSES
+QUAD = 32
+QUADS = P // QUAD
+SPLIT_LOADS = (0, 1, PASSES)
+
+
+def tile_mix_feat_fm_crelu_bias_kernel(tc, x, w4_words, w4_scales, w8_words, w8_scales, b, out):
+    nc = tc.nc
+    with ExitStack() as ctx:
+        keep = ctx.enter_context(tc.tile_pool(name="keep", bufs=1))
+        stage = ctx.enter_context(tc.tile_pool(name="stage", bufs=3))
+        psum = ctx.enter_context(tc.psum_pool(name="psum", bufs=1))
+        ctx.enter_context(tc.manual_schedule())
+
+        w8_plane = keep.tile([P, M], U8, name="w8_plane", align_bytes=64)
+        w4_plane = [keep.tile([P, M], U8, name="w4_plane%d" % a, align_bytes=64) for a in range(PASSES)]
+        w8_codes = [keep.tile([P, M], U32, name="w8_codes%d" % a, align_bytes=64) for a in range(PASSES)]
+        w4_codes = [keep.tile([P, 2 * M], U8, name="w4_codes%d" % a, align_bytes=64) for a in range(PASSES)]
+        bias_rows = keep.tile([P, M_TILES * QUAD], F32, name="bias_rows", align_bytes=64)
+        bias_cols = keep.tile([P, M_TILES * QUAD], F32, name="bias_cols", align_bytes=64)
+
+        nc.vector.memset(w8_plane[:].bitcast(U32), 0)
+        for a in range(PASSES):
+            nc.vector.memset(w4_plane[a][:].bitcast(U32), 0)
+        nc.vector.memset(bias_rows[:], 0.0)
+
+        raw = {}
+
+        def load_x(step, first_half, halves):
+            sweep, a = divmod(step, PASSES)
+            t0 = sweep * N + first_half * HALF
+            width = halves * HALF
+            rows = keep.tile([P, PACK, width], F32, name="x_raw%d_%d" % (step, first_half))
+            src = x[a * K_PASS : (a + 1) * K_PASS, t0 : t0 + width]
+            nc.sync.dma_start(out=rows[:], in_=src.rearrange("(p j) w -> p j w", j=PACK))
+            for u in range(halves):
+                raw[step, first_half + u] = rows[:, :, u * HALF : (u + 1) * HALF]
+
+        def load_x_step(step):
+            if step in SPLIT_LOADS:
+                load_x(step, 0, 1)
+                load_x(step, 1, 1)
+            else:
+                load_x(step, 0, 2)
+
+        def load_w8(a, n0, n1):
+            words = w8_words[a].rearrange("p n i -> p (n i)").bitcast(I32)
+            nc.sync.dma_start(out=w8_codes[a][:, n0:n1].bitcast(I32), in_=words[:, n0:n1])
+
+        def load_w4(a):
+            for r in range(PACK):
+                nc.sync.dma_start(
+                    out=w4_plane[a][r:P:QUAD, :].bitcast(I32),
+                    in_=w4_scales[a, r : 4 * PACK : PACK, :].bitcast(I32),
+                )
+            nc.sync.dma_start(out=w4_codes[a][:].bitcast(I32), in_=w4_words[a].bitcast(I32))
+
+        load_x(0, 0, 1)
+        for q in range(QUADS):
+            nc.sync.dma_start(
+                out=w8_plane[QUAD * q : QUAD * q + PASSES * PACK, :].bitcast(I32),
+                in_=w8_scales[:, PACK * q : PACK * (q + 1), :].bitcast(I32),
+            )
+        load_w8(0, 0, M // 2)
+        load_x(0, 1, 1)
+        load_w8(0, M // 2, M)
+        load_w4(0)
+        for a in range(1, PASSES):
+            load_x_step(a)
+            load_w8(a, 0, M)
+            load_w4(a)
+            if a == 1:
+                nc.sync.dma_start(
+                    out=bias_rows[0:P:QUAD, :].rearrange("q (m c) -> q m c", c=QUAD),
+                    in_=b.rearrange("(m q c) -> q m c", q=QUADS, c=QUAD),
+                )
+        for step in range(PASSES, STEPS):
+            load_x_step(step)
+
+        pos, neg = {}, {}
+
+        def new_operand(name, step):
+            values = stage.tile([P, N, PACK], BF16, name=name + "_bf16", align_bytes=64)
+            codes = keep.tile([P, N], U32, name="%s_codes%d" % (name, step), align_bytes=64)
+            scales = keep.tile([P, N], U8, name="%s_scales%d" % (name, step), align_bytes=64)
+            return values, codes, scales
+
+        def views(values, step, u):
+            dst = values[:, u * HALF : (u + 1) * HALF, :].rearrange("p (c i) j -> p c j i", i=4)
+            src = raw[step, u].rearrange("p j (c i) -> p c j i", i=4)
+            return dst, src
+
+        def neg_part(step, u):
+            dst, src = views(neg[step][0], step, u)
+            nc.vector.tensor_scalar(out=dst, in0=src, scalar1=-1.0, scalar2=0.0, op0=ALU.mult, op1=ALU.max)
+
+        def pos_part_vector(step, u):
+            dst, src = views(pos[step][0], step, u)
+            nc.vector.tensor_scalar(out=dst, in0=src, scalar1=0.0, scalar2=None, op0=ALU.max)
+
+        def pos_part_scalar(step, u):
+            dst, src = views(pos[step][0], step, u)
+            nc.scalar.activation(out=dst, in_=src, func=ACT.Relu)
+
+        def quantize(operand, c0, c1):
+            values, codes, scales = operand
+            nc.vector.quantize_mx(
+                out=codes[:, c0:c1].bitcast(FP8X4),
+                scales=scales[:, c0:c1],
+                in_=values[:, c0:c1, :].rearrange("p w j -> p (w j)"),
+            )
+
+        acc = {}
+
+        def w8_pass(step, m, c0, c1, start):
+            a = step % PASSES
+            cols = slice(m * P, (m + 1) * P)
+            nc.tensor.matmul_mx(
+                out=acc[m][:, c0:c1],
+                lhsT=w8_codes[a][:, cols].bitcast(FP8X4),
+                lhsT_scale=w8_plane[PACK * a : P, cols],
+                rhs=neg[step][1][:, c0:c1].bitcast(FP8X4),
+                rhs_scale=neg[step][2][:, c0:c1],
+                start=start,
+                stop=False,
+            )
+
+        def w4_pass(step, m):
+            a = step % PASSES
+            nc.tensor.matmul_mx(
+                out=acc[m][:],
+                lhsT=w4_codes[a][:, 2 * m * P : 2 * (m + 1) * P].bitcast(FP4X4),
+                lhsT_scale=w4_plane[a][:, m * P : (m + 1) * P],
+                rhs=pos[step][1][:].bitcast(FP8X4),
+                rhs_scale=pos[step][2][:],
+                start=False,
+                stop=(a == PASSES - 1),
+            )
+
+        def open_banks():
+            for m in range(M_TILES):
+                acc[m] = psum.tile([P, N], F32, name="acc%d" % m)
+
+        def drain(sweep, m, on_vector):
+            result = keep.tile([P, N], F32, name="result%d_%d" % (sweep, m))
+            bias = bias_cols[:, QUAD * m : QUAD * m + 1]
+            if on_vector:
+                nc.vector.tensor_scalar(out=result[:], in0=acc[m][:], scalar1=bias, scalar2=None, op0=ALU.add)
+            else:
+                nc.scalar.activation(out=result[:], in_=acc[m][:], func=ACT.Identity, bias=bias)
+            nc.sync.dma_start(out=out[m * P : (m + 1) * P, sweep * N : (sweep + 1) * N], in_=result[:])
+
+        def neg_by_halves(step):
+            neg[step] = new_operand("neg", step)
+            for u in range(2):
+                neg_part(step, u)
+                quantize(neg[step], u * HALF, (u + 1) * HALF)
+
+        open_banks()
+        for step in range(PASSES):
+            neg_by_halves(step)
+            pos[step] = new_operand("pos", step)
+            for u in range(2):
+                pos_part_scalar(step, u)
+            quantize(pos[step], 0, N)
+            if step == 2:
+                nc.vector.transpose(out=bias_cols[:], in_=bias_rows[:])
+            for u in range(2):
+                for m in range(M_TILES):
+                    w8_pass(step, m, u * HALF, (u + 1) * HALF, start=(step == 0 and u == 0))
+            for m in range(M_TILES):
+                w4_pass(step, m)
+
+        step = PASSES
+        neg_by_halves(step)
+        pos[step] = new_operand("pos", step)
+        for u in range(2):
+            pos_part_vector(step, u)
+        for m in range(M_TILES):
+            drain(0, m, on_vector=(m == M_TILES - 1))
+        quantize(pos[step], 0, N)
+        open_banks()
+
+        for step in range(PASSES, STEPS):
+            if step > PASSES:
+                neg[step] = new_operand("neg", step)
+                pos[step] = new_operand("pos", step)
+                for u in range(2):
+                    neg_part(step, u)
+                    pos_part_scalar(step, u)
+                quantize(neg[step], 0, N)
+                quantize(pos[step], 0, N)
+            if step < STEPS - 1:
+                for m in range(M_TILES):
+                    w8_pass(step, m, 0, N, start=(step == PASSES))
+            if step < STEPS - 2:
+                for m in range(M_TILES):
+                    w4_pass(step, m)
+        for m in range(M_TILES):
+            w4_pass(STEPS - 2, m)
+            w8_pass(STEPS - 1, m, 0, N, start=False)
+            w4_pass(STEPS - 1, m)
+            drain(1, m, on_vector=(m % 2 == 1))

@@ -22,11 +22,10 @@ PASSES = K // K_PASS
 M_TILES = M // P
 N = 512
 HALF = N // 2
-SWEEPS = T // N
-STEPS = SWEEPS * PASSES
 QUAD = 32
 QUADS = P // QUAD
-SPLIT_LOADS = (0, 1, PASSES)
+SCALE_ROWS = 4
+LAST = PASSES - 1
 
 
 def tile_mix_feat_fm_crelu_bias_kernel(tc, x, w4_words, w4_scales, w8_words, w8_scales, b, out):
@@ -38,94 +37,82 @@ def tile_mix_feat_fm_crelu_bias_kernel(tc, x, w4_words, w4_scales, w8_words, w8_
         ctx.enter_context(tc.manual_schedule())
 
         w8_plane = keep.tile([P, M], U8, name="w8_plane", align_bytes=64)
-        w4_plane = [keep.tile([P, M], U8, name="w4_plane%d" % a, align_bytes=64) for a in range(PASSES)]
+        w4_plane_first = keep.tile([P, M], U8, name="w4_plane_first", align_bytes=64)
+        w4_plane_rest = keep.tile([P, LAST * M], U8, name="w4_plane_rest", align_bytes=64)
+        w4_plane = [w4_plane_first[:]] + [w4_plane_rest[:, a * M : (a + 1) * M] for a in range(LAST)]
         w8_codes = [keep.tile([P, M], U32, name="w8_codes%d" % a, align_bytes=64) for a in range(PASSES)]
         w4_codes = [keep.tile([P, 2 * M], U8, name="w4_codes%d" % a, align_bytes=64) for a in range(PASSES)]
         bias_rows = keep.tile([P, M_TILES * QUAD], F32, name="bias_rows", align_bytes=64)
         bias_cols = keep.tile([P, M_TILES * QUAD], F32, name="bias_cols", align_bytes=64)
 
         nc.vector.memset(w8_plane[:].bitcast(U32), 0)
-        for a in range(PASSES):
-            nc.vector.memset(w4_plane[a][:].bitcast(U32), 0)
+        nc.vector.memset(w4_plane_first[:].bitcast(U32), 0)
+        nc.vector.memset(w4_plane_rest[:].bitcast(U32), 0)
         nc.vector.memset(bias_rows[:], 0.0)
 
         raw = {}
 
-        def load_x(step, first_half, halves):
-            sweep, a = divmod(step, PASSES)
-            t0 = sweep * N + first_half * HALF
+        def load_x(blk, a, first_half, halves):
+            t0 = blk * N + first_half * HALF
             width = halves * HALF
-            rows = keep.tile([P, PACK, width], F32, name="x_raw%d_%d" % (step, first_half))
+            rows = keep.tile([P, PACK, width], F32, name="x_raw%d_%d_%d" % (blk, a, first_half))
             src = x[a * K_PASS : (a + 1) * K_PASS, t0 : t0 + width]
             nc.sync.dma_start(out=rows[:], in_=src.rearrange("(p j) w -> p j w", j=PACK))
             for u in range(halves):
-                raw[step, first_half + u] = rows[:, :, u * HALF : (u + 1) * HALF]
-
-        def load_x_step(step):
-            if step in SPLIT_LOADS:
-                load_x(step, 0, 1)
-                load_x(step, 1, 1)
-            else:
-                load_x(step, 0, 2)
+                raw[blk, a, first_half + u] = rows[:, :, u * HALF : (u + 1) * HALF]
 
         def load_w8(a, n0, n1):
             words = w8_words[a].rearrange("p n i -> p (n i)").bitcast(I32)
             nc.sync.dma_start(out=w8_codes[a][:, n0:n1].bitcast(I32), in_=words[:, n0:n1])
 
         def load_w4(a):
-            for r in range(PACK):
-                nc.sync.dma_start(
-                    out=w4_plane[a][r:P:QUAD, :].bitcast(I32),
-                    in_=w4_scales[a, r : 4 * PACK : PACK, :].bitcast(I32),
-                )
             nc.sync.dma_start(out=w4_codes[a][:].bitcast(I32), in_=w4_words[a].bitcast(I32))
 
-        load_x(0, 0, 1)
+        def load_w4_scales(plane, a0, a1):
+            for r in range(SCALE_ROWS):
+                nc.sync.dma_start(
+                    out=plane[r:P:QUAD, :].bitcast(I32).rearrange("q (a n) -> q a n", a=a1 - a0),
+                    in_=w4_scales[a0:a1, r : QUADS * SCALE_ROWS : SCALE_ROWS, :].bitcast(I32).rearrange("a q n -> q a n"),
+                )
+
+        load_x(0, 0, 0, 1)
         for q in range(QUADS):
             nc.sync.dma_start(
-                out=w8_plane[QUAD * q : QUAD * q + PASSES * PACK, :].bitcast(I32),
-                in_=w8_scales[:, PACK * q : PACK * (q + 1), :].bitcast(I32),
+                out=w8_plane[QUAD * q : QUAD * q + PASSES * SCALE_ROWS, :].bitcast(I32),
+                in_=w8_scales[:, SCALE_ROWS * q : SCALE_ROWS * (q + 1), :].bitcast(I32),
             )
         load_w8(0, 0, M // 2)
-        load_x(0, 1, 1)
+        load_x(0, 0, 1, 1)
         load_w8(0, M // 2, M)
+        load_w4_scales(w4_plane_first, 0, 1)
         load_w4(0)
+        load_x(1, 0, 0, 1)
+        load_x(1, 0, 1, 1)
         for a in range(1, PASSES):
-            load_x_step(a)
+            load_x(1, a, 0, 2)
             load_w8(a, 0, M)
-            load_w4(a)
             if a == 1:
+                load_w4_scales(w4_plane_rest, 1, PASSES)
                 nc.sync.dma_start(
                     out=bias_rows[0:P:QUAD, :].rearrange("q (m c) -> q m c", c=QUAD),
                     in_=b.rearrange("(m q c) -> q m c", q=QUADS, c=QUAD),
                 )
-        for step in range(PASSES, STEPS):
-            load_x_step(step)
+            load_w4(a)
+        for a in range(1, PASSES):
+            load_x(0, a, 0, 2)
+
+        def new_operand(name, blk, a):
+            values = stage.tile([P, N, PACK], BF16, name=name + "_bf16", align_bytes=64)
+            codes = keep.tile([P, N], U32, name="%s_codes%d_%d" % (name, blk, a), align_bytes=64)
+            scales = keep.tile([P, N], U8, name="%s_scales%d_%d" % (name, blk, a), align_bytes=64)
+            return values, codes, scales
 
         pos, neg = {}, {}
 
-        def new_operand(name, step):
-            values = stage.tile([P, N, PACK], BF16, name=name + "_bf16", align_bytes=64)
-            codes = keep.tile([P, N], U32, name="%s_codes%d" % (name, step), align_bytes=64)
-            scales = keep.tile([P, N], U8, name="%s_scales%d" % (name, step), align_bytes=64)
-            return values, codes, scales
-
-        def views(values, step, u):
+        def views(values, blk, a, u):
             dst = values[:, u * HALF : (u + 1) * HALF, :].rearrange("p (c i) j -> p c j i", i=4)
-            src = raw[step, u].rearrange("p j (c i) -> p c j i", i=4)
+            src = raw[blk, a, u].rearrange("p j (c i) -> p c j i", i=4)
             return dst, src
-
-        def neg_part(step, u):
-            dst, src = views(neg[step][0], step, u)
-            nc.vector.tensor_scalar(out=dst, in0=src, scalar1=-1.0, scalar2=0.0, op0=ALU.mult, op1=ALU.max)
-
-        def pos_part_vector(step, u):
-            dst, src = views(pos[step][0], step, u)
-            nc.vector.tensor_scalar(out=dst, in0=src, scalar1=0.0, scalar2=None, op0=ALU.max)
-
-        def pos_part_scalar(step, u):
-            dst, src = views(pos[step][0], step, u)
-            nc.scalar.activation(out=dst, in_=src, func=ACT.Relu)
 
         def quantize(operand, c0, c1):
             values, codes, scales = operand
@@ -135,94 +122,120 @@ def tile_mix_feat_fm_crelu_bias_kernel(tc, x, w4_words, w4_scales, w8_words, w8_
                 in_=values[:, c0:c1, :].rearrange("p w j -> p (w j)"),
             )
 
+        def make_neg(blk, a):
+            neg[blk, a] = new_operand("neg", blk, a)
+            for u in range(2):
+                dst, src = views(neg[blk, a][0], blk, a, u)
+                nc.vector.tensor_scalar(out=dst, in0=src, scalar1=-1.0, scalar2=0.0, op0=ALU.mult, op1=ALU.max)
+                quantize(neg[blk, a], u * HALF, (u + 1) * HALF)
+
+        def make_pos(blk, a, on_vector):
+            pos[blk, a] = new_operand("pos", blk, a)
+            for u in range(2):
+                dst, src = views(pos[blk, a][0], blk, a, u)
+                if on_vector:
+                    nc.vector.tensor_scalar(out=dst, in0=src, scalar1=0.0, scalar2=None, op0=ALU.max)
+                else:
+                    nc.scalar.activation(out=dst, in_=src, func=ACT.Relu)
+            quantize(pos[blk, a], 0, N)
+
         acc = {}
-
-        def w8_pass(step, m, c0, c1, start):
-            a = step % PASSES
-            cols = slice(m * P, (m + 1) * P)
-            nc.tensor.matmul_mx(
-                out=acc[m][:, c0:c1],
-                lhsT=w8_codes[a][:, cols].bitcast(FP8X4),
-                lhsT_scale=w8_plane[PACK * a : P, cols],
-                rhs=neg[step][1][:, c0:c1].bitcast(FP8X4),
-                rhs_scale=neg[step][2][:, c0:c1],
-                start=start,
-                stop=False,
-            )
-
-        def w4_pass(step, m):
-            a = step % PASSES
-            nc.tensor.matmul_mx(
-                out=acc[m][:],
-                lhsT=w4_codes[a][:, 2 * m * P : 2 * (m + 1) * P].bitcast(FP4X4),
-                lhsT_scale=w4_plane[a][:, m * P : (m + 1) * P],
-                rhs=pos[step][1][:].bitcast(FP8X4),
-                rhs_scale=pos[step][2][:],
-                start=False,
-                stop=(a == PASSES - 1),
-            )
 
         def open_banks():
             for m in range(M_TILES):
                 acc[m] = psum.tile([P, N], F32, name="acc%d" % m)
 
-        def drain(sweep, m, on_vector):
-            result = keep.tile([P, N], F32, name="result%d_%d" % (sweep, m))
-            bias = bias_cols[:, QUAD * m : QUAD * m + 1]
-            if on_vector:
-                nc.vector.tensor_scalar(out=result[:], in0=acc[m][:], scalar1=bias, scalar2=None, op0=ALU.add)
-            else:
-                nc.scalar.activation(out=result[:], in_=acc[m][:], func=ACT.Identity, bias=bias)
-            nc.sync.dma_start(out=out[m * P : (m + 1) * P, sweep * N : (sweep + 1) * N], in_=result[:])
+        def w8_pass(blk, a, m, c0, c1, start=False):
+            cols = slice(m * P, (m + 1) * P)
+            nc.tensor.matmul_mx(
+                out=acc[m][:, c0:c1],
+                lhsT=w8_codes[a][:, cols].bitcast(FP8X4),
+                lhsT_scale=w8_plane[SCALE_ROWS * a : P, cols],
+                rhs=neg[blk, a][1][:, c0:c1].bitcast(FP8X4),
+                rhs_scale=neg[blk, a][2][:, c0:c1],
+                start=start,
+                stop=False,
+            )
 
-        def neg_by_halves(step):
-            neg[step] = new_operand("neg", step)
-            for u in range(2):
-                neg_part(step, u)
-                quantize(neg[step], u * HALF, (u + 1) * HALF)
+        def w4_pass(blk, a, m, stop=False):
+            nc.tensor.matmul_mx(
+                out=acc[m][:],
+                lhsT=w4_codes[a][:, 2 * m * P : 2 * (m + 1) * P].bitcast(FP4X4),
+                lhsT_scale=w4_plane[a][:, m * P : (m + 1) * P],
+                rhs=pos[blk, a][1][:].bitcast(FP8X4),
+                rhs_scale=pos[blk, a][2][:],
+                start=False,
+                stop=stop,
+            )
+
+        def w8_half_passes(blk, a, u, tiles, start=False):
+            for m in tiles:
+                w8_pass(blk, a, m, u * HALF, (u + 1) * HALF, start=start)
+
+        def store(blk, m, result):
+            nc.sync.dma_start(out=out[m * P : (m + 1) * P, blk * N : (blk + 1) * N], in_=result[:])
+
+        every = range(M_TILES)
+        lower, upper = range(M_TILES // 2), range(M_TILES // 2, M_TILES)
 
         open_banks()
-        for step in range(PASSES):
-            neg_by_halves(step)
-            pos[step] = new_operand("pos", step)
-            for u in range(2):
-                pos_part_scalar(step, u)
-            quantize(pos[step], 0, N)
-            if step == 2:
-                nc.vector.transpose(out=bias_cols[:], in_=bias_rows[:])
-            for u in range(2):
-                for m in range(M_TILES):
-                    w8_pass(step, m, u * HALF, (u + 1) * HALF, start=(step == 0 and u == 0))
-            for m in range(M_TILES):
-                w4_pass(step, m)
+        make_neg(0, 0)
+        make_pos(0, 0, on_vector=False)
+        w8_half_passes(0, 0, 0, every, start=True)
+        w8_half_passes(0, 0, 1, every)
+        partial = {}
+        for m in every:
+            w4_pass(0, 0, m, stop=True)
+            partial[m] = keep.tile([P, N], F32, name="partial%d" % m)
+            nc.scalar.copy(out=partial[m][:], in_=acc[m][:])
 
-        step = PASSES
-        neg_by_halves(step)
-        pos[step] = new_operand("pos", step)
-        for u in range(2):
-            pos_part_vector(step, u)
-        for m in range(M_TILES):
-            drain(0, m, on_vector=(m == M_TILES - 1))
-        quantize(pos[step], 0, N)
         open_banks()
+        make_neg(1, 0)
+        make_pos(1, 0, on_vector=True)
+        w8_half_passes(1, 0, 0, lower, start=True)
+        w8_half_passes(1, 0, 1, lower)
+        for m in upper:
+            w8_pass(1, 0, m, 0, N, start=True)
+        for m in every:
+            w4_pass(1, 0, m)
+        for a in range(1, PASSES):
+            make_neg(1, a)
+            make_pos(1, a, on_vector=False)
+            w8_half_passes(1, a, 0, every)
+            if a < LAST:
+                w8_half_passes(1, a, 1, every)
+                for m in every:
+                    w4_pass(1, a, m)
+        nc.vector.transpose(out=bias_cols[:], in_=bias_rows[:])
+        for m in every:
+            w8_pass(1, LAST, m, HALF, N)
+            w4_pass(1, LAST, m, stop=True)
+            result = keep.tile([P, N], F32, name="result%d" % m)
+            nc.scalar.activation(
+                out=result[:], in_=acc[m][:], func=ACT.Identity, bias=bias_cols[:, QUAD * m : QUAD * m + 1]
+            )
+            store(1, m, result)
 
-        for step in range(PASSES, STEPS):
-            if step > PASSES:
-                neg[step] = new_operand("neg", step)
-                pos[step] = new_operand("pos", step)
-                for u in range(2):
-                    neg_part(step, u)
-                    pos_part_scalar(step, u)
-                quantize(neg[step], 0, N)
-                quantize(pos[step], 0, N)
-            if step < STEPS - 1:
-                for m in range(M_TILES):
-                    w8_pass(step, m, 0, N, start=(step == PASSES))
-            if step < STEPS - 2:
-                for m in range(M_TILES):
-                    w4_pass(step, m)
-        for m in range(M_TILES):
-            w4_pass(STEPS - 2, m)
-            w8_pass(STEPS - 1, m, 0, N, start=False)
-            w4_pass(STEPS - 1, m)
-            drain(1, m, on_vector=(m % 2 == 1))
+        open_banks()
+        for a in range(1, PASSES):
+            make_neg(0, a)
+            make_pos(0, a, on_vector=(a == 1))
+        for m in every:
+            w8_pass(0, 1, m, 0, N, start=True)
+        for m in every:
+            w4_pass(0, 1, m)
+        for m in every:
+            w8_pass(0, 2, m, 0, N)
+        for m in every:
+            w4_pass(0, 2, m)
+            w8_pass(0, LAST, m, 0, N)
+            w4_pass(0, LAST, m, stop=True)
+            nc.vector.scalar_tensor_tensor(
+                out=partial[m][:],
+                in0=acc[m][:],
+                scalar=bias_cols[:, QUAD * m : QUAD * m + 1],
+                in1=partial[m][:],
+                op0=ALU.add,
+                op1=ALU.add,
+            )
+            store(0, m, partial[m])

@@ -26,6 +26,8 @@ QUAD = 32
 QUADS = P // QUAD
 SCALE_ROWS = 4
 LAST = PASSES - 1
+WARM_PASSES = 20
+EARLY_BANKS = 6
 
 
 def tile_mix_feat_fm_crelu_bias_kernel(tc, x, w4_words, w4_scales, w8_words, w8_scales, b, out):
@@ -46,7 +48,23 @@ def tile_mix_feat_fm_crelu_bias_kernel(tc, x, w4_words, w4_scales, w8_words, w8_
         bias_cols = keep.tile([P, M_TILES * QUAD], F32, name="bias_cols", align_bytes=64)
 
         nc.vector.memset(w8_plane[:].bitcast(U32), 0)
+        warm_values = keep.tile([P, PACK * P], BF16, name="warm_values", align_bytes=64)
+        warm_codes = keep.tile([P, P], U32, name="warm_codes", align_bytes=64)
+        warm_scales = keep.tile([P, P], U8, name="warm_scales", align_bytes=64)
+        nc.vector.memset(warm_values[:], 1.0)
         nc.vector.memset(w4_plane_first[:].bitcast(U32), 0)
+        nc.vector.quantize_mx(out=warm_codes[:].bitcast(FP8X4), scales=warm_scales[:], in_=warm_values[:])
+        warm_out = psum.tile([P, N], F32, name="acc%d" % (M_TILES - 1))
+        for i in range(WARM_PASSES):
+            nc.tensor.matmul_mx(
+                out=warm_out[:, 0:P],
+                lhsT=warm_codes[:].bitcast(FP8X4),
+                lhsT_scale=warm_scales[:],
+                rhs=warm_codes[:].bitcast(FP8X4),
+                rhs_scale=warm_scales[:],
+                start=True,
+                stop=True,
+            )
         nc.vector.memset(w4_plane_rest[:].bitcast(U32), 0)
         nc.vector.memset(bias_rows[:], 0.0)
 
@@ -122,22 +140,28 @@ def tile_mix_feat_fm_crelu_bias_kernel(tc, x, w4_words, w4_scales, w8_words, w8_
                 in_=values[:, c0:c1, :].rearrange("p w j -> p (w j)"),
             )
 
-        def make_neg(blk, a):
-            neg[blk, a] = new_operand("neg", blk, a)
-            for u in range(2):
-                dst, src = views(neg[blk, a][0], blk, a, u)
-                nc.vector.tensor_scalar(out=dst, in0=src, scalar1=-1.0, scalar2=0.0, op0=ALU.mult, op1=ALU.max)
-                quantize(neg[blk, a], u * HALF, (u + 1) * HALF)
+        def neg_half(blk, a, u):
+            dst, src = views(neg[blk, a][0], blk, a, u)
+            nc.vector.tensor_scalar(out=dst, in0=src, scalar1=-1.0, scalar2=0.0, op0=ALU.mult, op1=ALU.max)
 
-        def make_pos(blk, a, on_vector):
+        def pos_half(blk, a, u, on_vector):
+            dst, src = views(pos[blk, a][0], blk, a, u)
+            if on_vector:
+                nc.vector.tensor_scalar(out=dst, in0=src, scalar1=0.0, scalar2=None, op0=ALU.max)
+            else:
+                nc.scalar.activation(out=dst, in_=src, func=ACT.Relu)
+
+        def make_operands(blk, a, pos_on_vector):
+            neg[blk, a] = new_operand("neg", blk, a)
             pos[blk, a] = new_operand("pos", blk, a)
-            for u in range(2):
-                dst, src = views(pos[blk, a][0], blk, a, u)
-                if on_vector:
-                    nc.vector.tensor_scalar(out=dst, in0=src, scalar1=0.0, scalar2=None, op0=ALU.max)
-                else:
-                    nc.scalar.activation(out=dst, in_=src, func=ACT.Relu)
-            quantize(pos[blk, a], 0, N)
+            neg_half(blk, a, 0)
+            pos_half(blk, a, 0, pos_on_vector)
+            quantize(neg[blk, a], 0, HALF)
+            neg_half(blk, a, 1)
+            quantize(pos[blk, a], 0, HALF)
+            quantize(neg[blk, a], HALF, N)
+            pos_half(blk, a, 1, pos_on_vector)
+            quantize(pos[blk, a], HALF, N)
 
         acc = {}
 
@@ -172,35 +196,34 @@ def tile_mix_feat_fm_crelu_bias_kernel(tc, x, w4_words, w4_scales, w8_words, w8_
             for m in tiles:
                 w8_pass(blk, a, m, u * HALF, (u + 1) * HALF, start=start)
 
-        def store(blk, m, result):
-            nc.sync.dma_start(out=out[m * P : (m + 1) * P, blk * N : (blk + 1) * N], in_=result[:])
+        def store(blk, m, result, c0, c1):
+            nc.sync.dma_start(out=out[m * P : (m + 1) * P, blk * N + c0 : blk * N + c1], in_=result[:, c0:c1])
 
         every = range(M_TILES)
         lower, upper = range(M_TILES // 2), range(M_TILES // 2, M_TILES)
 
         open_banks()
-        make_neg(0, 0)
-        make_pos(0, 0, on_vector=False)
+        make_operands(0, 0, pos_on_vector=False)
         w8_half_passes(0, 0, 0, every, start=True)
-        w8_half_passes(0, 0, 1, every)
+        w8_half_passes(0, 0, 1, lower)
         partial = {}
         for m in every:
+            if m in upper:
+                w8_pass(0, 0, m, HALF, N)
             w4_pass(0, 0, m, stop=True)
             partial[m] = keep.tile([P, N], F32, name="partial%d" % m)
             nc.scalar.copy(out=partial[m][:], in_=acc[m][:])
 
         open_banks()
-        make_neg(1, 0)
-        make_pos(1, 0, on_vector=True)
-        w8_half_passes(1, 0, 0, lower, start=True)
-        w8_half_passes(1, 0, 1, lower)
-        for m in upper:
+        make_operands(1, 0, pos_on_vector=True)
+        w8_half_passes(1, 0, 0, range(EARLY_BANKS), start=True)
+        w8_half_passes(1, 0, 1, range(EARLY_BANKS))
+        for m in range(EARLY_BANKS, M_TILES):
             w8_pass(1, 0, m, 0, N, start=True)
         for m in every:
             w4_pass(1, 0, m)
         for a in range(1, PASSES):
-            make_neg(1, a)
-            make_pos(1, a, on_vector=False)
+            make_operands(1, a, pos_on_vector=False)
             w8_half_passes(1, a, 0, every)
             if a < LAST:
                 w8_half_passes(1, a, 1, every)
@@ -214,12 +237,11 @@ def tile_mix_feat_fm_crelu_bias_kernel(tc, x, w4_words, w4_scales, w8_words, w8_
             nc.scalar.activation(
                 out=result[:], in_=acc[m][:], func=ACT.Identity, bias=bias_cols[:, QUAD * m : QUAD * m + 1]
             )
-            store(1, m, result)
+            store(1, m, result, 0, N)
 
         open_banks()
         for a in range(1, PASSES):
-            make_neg(0, a)
-            make_pos(0, a, on_vector=(a == 1))
+            make_operands(0, a, pos_on_vector=(a == 1))
         for m in every:
             w8_pass(0, 1, m, 0, N, start=True)
         for m in every:
@@ -230,12 +252,14 @@ def tile_mix_feat_fm_crelu_bias_kernel(tc, x, w4_words, w4_scales, w8_words, w8_
             w4_pass(0, 2, m)
             w8_pass(0, LAST, m, 0, N)
             w4_pass(0, LAST, m, stop=True)
-            nc.vector.scalar_tensor_tensor(
-                out=partial[m][:],
-                in0=acc[m][:],
-                scalar=bias_cols[:, QUAD * m : QUAD * m + 1],
-                in1=partial[m][:],
-                op0=ALU.add,
-                op1=ALU.add,
-            )
-            store(0, m, partial[m])
+            width = HALF if m == M_TILES - 1 else N
+            for c0 in range(0, N, width):
+                nc.vector.scalar_tensor_tensor(
+                    out=partial[m][:, c0 : c0 + width],
+                    in0=acc[m][:, c0 : c0 + width],
+                    scalar=bias_cols[:, QUAD * m : QUAD * m + 1],
+                    in1=partial[m][:, c0 : c0 + width],
+                    op0=ALU.add,
+                    op1=ALU.add,
+                )
+                store(0, m, partial[m], c0, c0 + width)

from contextlib import ExitStack

import concourse.mybir as mybir

K, M, T = 2048, 1024, 1024
FLOPS = 2 * 2 * K * M * T

F32 = mybir.dt.float32
BF16 = mybir.dt.bfloat16
I32 = mybir.dt.int32
U32 = mybir.dt.uint32
U8 = mybir.dt.uint8
FP8X4 = mybir.dt.float8_e4m3fn_x4
FP4X4 = mybir.dt.float4_e2m1fn_x4
ALU = mybir.AluOpType
ACT = mybir.ActivationFunctionType

P = 128
PACK = 4
K_PASS = P * PACK
PASSES = K // K_PASS
M_TILES = M // P
N = 512
HALF = N // 2
QUAD = 32
QUADS = P // QUAD
SCALE_ROWS = 4
LAST = PASSES - 1
WARM_PASSES = 20
EARLY_BANKS = 6


def tile_mix_feat_fm_crelu_bias_kernel(tc, x, w4_words, w4_scales, w8_words, w8_scales, b, out):
    nc = tc.nc
    with ExitStack() as ctx:
        keep = ctx.enter_context(tc.tile_pool(name="keep", bufs=1))
        stage = ctx.enter_context(tc.tile_pool(name="stage", bufs=3))
        psum = ctx.enter_context(tc.psum_pool(name="psum", bufs=1))
        ctx.enter_context(tc.manual_schedule())

        w8_plane = keep.tile([P, M], U8, name="w8_plane", align_bytes=64)
        w4_plane_first = keep.tile([P, M], U8, name="w4_plane_first", align_bytes=64)
        w4_plane_rest = keep.tile([P, LAST * M], U8, name="w4_plane_rest", align_bytes=64)
        w4_plane = [w4_plane_first[:]] + [w4_plane_rest[:, a * M : (a + 1) * M] for a in range(LAST)]
        w8_codes = [keep.tile([P, M], U32, name="w8_codes%d" % a, align_bytes=64) for a in range(PASSES)]
        w4_codes = [keep.tile([P, 2 * M], U8, name="w4_codes%d" % a, align_bytes=64) for a in range(PASSES)]
        bias_rows = keep.tile([P, M_TILES * QUAD], F32, name="bias_rows", align_bytes=64)
        bias_cols = keep.tile([P, M_TILES * QUAD], F32, name="bias_cols", align_bytes=64)

        nc.vector.memset(w8_plane[:].bitcast(U32), 0)
        warm_values = keep.tile([P, PACK * P], BF16, name="warm_values", align_bytes=64)
        warm_codes = keep.tile([P, P], U32, name="warm_codes", align_bytes=64)
        warm_scales = keep.tile([P, P], U8, name="warm_scales", align_bytes=64)
        nc.vector.memset(warm_values[:], 1.0)
        nc.vector.memset(w4_plane_first[:].bitcast(U32), 0)
        nc.vector.quantize_mx(out=warm_codes[:].bitcast(FP8X4), scales=warm_scales[:], in_=warm_values[:])
        warm_out = psum.tile([P, N], F32, name="acc%d" % (M_TILES - 1))
        for i in range(WARM_PASSES):
            nc.tensor.matmul_mx(
                out=warm_out[:, 0:P],
                lhsT=warm_codes[:].bitcast(FP8X4),
                lhsT_scale=warm_scales[:],
                rhs=warm_codes[:].bitcast(FP8X4),
                rhs_scale=warm_scales[:],
                start=True,
                stop=True,
            )
        nc.vector.memset(w4_plane_rest[:].bitcast(U32), 0)
        nc.vector.memset(bias_rows[:], 0.0)

        raw = {}

        def load_x(blk, a, first_half, halves):
            t0 = blk * N + first_half * HALF
            width = halves * HALF
            rows = keep.tile([P, PACK, width], F32, name="x_raw%d_%d_%d" % (blk, a, first_half))
            src = x[a * K_PASS : (a + 1) * K_PASS, t0 : t0 + width]
            nc.sync.dma_start(out=rows[:], in_=src.rearrange("(p j) w -> p j w", j=PACK))
            for u in range(halves):
                raw[blk, a, first_half + u] = rows[:, :, u * HALF : (u + 1) * HALF]

        def load_w8(a, n0, n1):
            words = w8_words[a].rearrange("p n i -> p (n i)").bitcast(I32)
            nc.sync.dma_start(out=w8_codes[a][:, n0:n1].bitcast(I32), in_=words[:, n0:n1])

        def load_w4(a):
            nc.sync.dma_start(out=w4_codes[a][:].bitcast(I32), in_=w4_words[a].bitcast(I32))

        def load_w4_scales(plane, a0, a1):
            for r in range(SCALE_ROWS):
                nc.sync.dma_start(
                    out=plane[r:P:QUAD, :].bitcast(I32).rearrange("q (a n) -> q a n", a=a1 - a0),
                    in_=w4_scales[a0:a1, r : QUADS * SCALE_ROWS : SCALE_ROWS, :].bitcast(I32).rearrange("a q n -> q a n"),
                )

        load_x(0, 0, 0, 1)
        for q in range(QUADS):
            nc.sync.dma_start(
                out=w8_plane[QUAD * q : QUAD * q + PASSES * SCALE_ROWS, :].bitcast(I32),
                in_=w8_scales[:, SCALE_ROWS * q : SCALE_ROWS * (q + 1), :].bitcast(I32),
            )
        load_w8(0, 0, M // 2)
        load_x(0, 0, 1, 1)
        load_w8(0, M // 2, M)
        load_w4_scales(w4_plane_first, 0, 1)
        load_w4(0)
        load_x(1, 0, 0, 1)
        load_x(1, 0, 1, 1)
        for a in range(1, PASSES):
            load_x(1, a, 0, 2)
            load_w8(a, 0, M)
            if a == 1:
                load_w4_scales(w4_plane_rest, 1, PASSES)
                nc.sync.dma_start(
                    out=bias_rows[0:P:QUAD, :].rearrange("q (m c) -> q m c", c=QUAD),
                    in_=b.rearrange("(m q c) -> q m c", q=QUADS, c=QUAD),
                )
            load_w4(a)
        for a in range(1, PASSES):
            load_x(0, a, 0, 2)

        def new_operand(name, blk, a):
            values = stage.tile([P, N, PACK], BF16, name=name + "_bf16", align_bytes=64)
            codes = keep.tile([P, N], U32, name="%s_codes%d_%d" % (name, blk, a), align_bytes=64)
            scales = keep.tile([P, N], U8, name="%s_scales%d_%d" % (name, blk, a), align_bytes=64)
            return values, codes, scales

        pos, neg = {}, {}

        def views(values, blk, a, u):
            dst = values[:, u * HALF : (u + 1) * HALF, :].rearrange("p (c i) j -> p c j i", i=4)
            src = raw[blk, a, u].rearrange("p j (c i) -> p c j i", i=4)
            return dst, src

        def quantize(operand, c0, c1):
            values, codes, scales = operand
            nc.vector.quantize_mx(
                out=codes[:, c0:c1].bitcast(FP8X4),
                scales=scales[:, c0:c1],
                in_=values[:, c0:c1, :].rearrange("p w j -> p (w j)"),
            )

        def neg_half(blk, a, u):
            dst, src = views(neg[blk, a][0], blk, a, u)
            nc.vector.tensor_scalar(out=dst, in0=src, scalar1=-1.0, scalar2=0.0, op0=ALU.mult, op1=ALU.max)

        def pos_half(blk, a, u, on_vector):
            dst, src = views(pos[blk, a][0], blk, a, u)
            if on_vector:
                nc.vector.tensor_scalar(out=dst, in0=src, scalar1=0.0, scalar2=None, op0=ALU.max)
            else:
                nc.scalar.activation(out=dst, in_=src, func=ACT.Relu)

        def make_operands(blk, a, pos_on_vector):
            neg[blk, a] = new_operand("neg", blk, a)
            pos[blk, a] = new_operand("pos", blk, a)
            neg_half(blk, a, 0)
            pos_half(blk, a, 0, pos_on_vector)
            quantize(neg[blk, a], 0, HALF)
            neg_half(blk, a, 1)
            quantize(pos[blk, a], 0, HALF)
            quantize(neg[blk, a], HALF, N)
            pos_half(blk, a, 1, pos_on_vector)
            quantize(pos[blk, a], HALF, N)

        acc = {}

        def open_banks():
            for m in range(M_TILES):
                acc[m] = psum.tile([P, N], F32, name="acc%d" % m)

        def w8_pass(blk, a, m, c0, c1, start=False):
            cols = slice(m * P, (m + 1) * P)
            nc.tensor.matmul_mx(
                out=acc[m][:, c0:c1],
                lhsT=w8_codes[a][:, cols].bitcast(FP8X4),
                lhsT_scale=w8_plane[SCALE_ROWS * a : P, cols],
                rhs=neg[blk, a][1][:, c0:c1].bitcast(FP8X4),
                rhs_scale=neg[blk, a][2][:, c0:c1],
                start=start,
                stop=False,
            )

        def w4_pass(blk, a, m, stop=False):
            nc.tensor.matmul_mx(
                out=acc[m][:],
                lhsT=w4_codes[a][:, 2 * m * P : 2 * (m + 1) * P].bitcast(FP4X4),
                lhsT_scale=w4_plane[a][:, m * P : (m + 1) * P],
                rhs=pos[blk, a][1][:].bitcast(FP8X4),
                rhs_scale=pos[blk, a][2][:],
                start=False,
                stop=stop,
            )

        def w8_half_passes(blk, a, u, tiles, start=False):
            for m in tiles:
                w8_pass(blk, a, m, u * HALF, (u + 1) * HALF, start=start)

        def store(blk, m, result, c0, c1):
            nc.sync.dma_start(out=out[m * P : (m + 1) * P, blk * N + c0 : blk * N + c1], in_=result[:, c0:c1])

        every = range(M_TILES)
        lower, upper = range(M_TILES // 2), range(M_TILES // 2, M_TILES)

        open_banks()
        make_operands(0, 0, pos_on_vector=False)
        w8_half_passes(0, 0, 0, every, start=True)
        w8_half_passes(0, 0, 1, lower)
        partial = {}
        for m in every:
            if m in upper:
                w8_pass(0, 0, m, HALF, N)
            w4_pass(0, 0, m, stop=True)
            partial[m] = keep.tile([P, N], F32, name="partial%d" % m)
            nc.scalar.copy(out=partial[m][:], in_=acc[m][:])

        open_banks()
        make_operands(1, 0, pos_on_vector=True)
        w8_half_passes(1, 0, 0, range(EARLY_BANKS), start=True)
        w8_half_passes(1, 0, 1, range(EARLY_BANKS))
        for m in range(EARLY_BANKS, M_TILES):
            w8_pass(1, 0, m, 0, N, start=True)
        for m in every:
            w4_pass(1, 0, m)
        for a in range(1, PASSES):
            make_operands(1, a, pos_on_vector=False)
            w8_half_passes(1, a, 0, every)
            if a < LAST:
                w8_half_passes(1, a, 1, every)
                for m in every:
                    w4_pass(1, a, m)
        nc.vector.transpose(out=bias_cols[:], in_=bias_rows[:])
        for m in every:
            w8_pass(1, LAST, m, HALF, N)
            w4_pass(1, LAST, m, stop=True)
            result = keep.tile([P, N], F32, name="result%d" % m)
            nc.scalar.activation(
                out=result[:], in_=acc[m][:], func=ACT.Identity, bias=bias_cols[:, QUAD * m : QUAD * m + 1]
            )
            store(1, m, result, 0, N)

        open_banks()
        for a in range(1, PASSES):
            make_operands(0, a, pos_on_vector=(a == 1))
        for m in every:
            w8_pass(0, 1, m, 0, N, start=True)
        for m in every:
            w4_pass(0, 1, m)
        for m in every:
            w8_pass(0, 2, m, 0, N)
        for m in every:
            w4_pass(0, 2, m)
            w8_pass(0, LAST, m, 0, N)
            w4_pass(0, LAST, m, stop=True)
            width = HALF if m == M_TILES - 1 else N
            for c0 in range(0, N, width):
                nc.vector.scalar_tensor_tensor(
                    out=partial[m][:, c0 : c0 + width],
                    in0=acc[m][:, c0 : c0 + width],
                    scalar=bias_cols[:, QUAD * m : QUAD * m + 1],
                    in1=partial[m][:, c0 : c0 + width],
                    op0=ALU.add,
                    op1=ALU.add,
                )
                store(0, m, partial[m], c0, c0 + width)
